import numpy as np
import ml_dtypes


def mxq(x, axis, fmt="e4m3"):
    dtype, down = {"e4m3": (ml_dtypes.float8_e4m3fn, 7), "e5m2": (ml_dtypes.float8_e5m2, 14)}[fmt]
    v = np.moveaxis(np.asarray(x, np.float32).astype(ml_dtypes.bfloat16).astype(np.float64), axis, -1)
    blocks = v.reshape(v.shape[:-1] + (-1, 32))
    amax = np.abs(blocks).max(-1, keepdims=True)
    byte = np.maximum(np.where(amax > 0, np.frexp(amax)[1] - 1 + 127, 0) - down, 1)
    scale = np.exp2(byte - 127.0)
    codes = (blocks / scale).astype(np.float32).astype(dtype).astype(np.float64)
    return np.moveaxis((codes * scale).reshape(v.shape), -1, axis)


WIDE = False


def mx_kscale(k):
    if not WIDE:
        return np.ones(k)
    levels = np.array([10, -10, 5, -5, 0])
    if k % 512:
        return np.exp2(np.random.permutation(np.resize(levels, k // 32))).repeat(32)
    a = np.empty((k // 512, 16))
    for p in range(k // 512):
        a[p, :8] = np.random.permutation(np.resize(levels, 8))
        for g in range(8):
            far = levels[np.abs(levels - a[p, g]) >= 10]
            a[p, g + 8] = far[np.random.randint(len(far))]
    return np.exp2(a.ravel()).repeat(32)


BF16 = ml_dtypes.bfloat16


def bf(x):
    return np.asarray(x, np.float32).astype(BF16)


def f64(x):
    return np.asarray(x).astype(np.float64)


E2M1 = np.array([0.0, 0.5, 1.0, 1.5, 2.0, 3.0, 4.0, 6.0, -0.0, -0.5, -1.0, -1.5, -2.0, -3.0, -4.0, -6.0])


def pack_weight(w, fmt):
    k, n = w.shape
    w = f64(bf(w)).reshape(k // 32, 32, n)
    amax = np.abs(w).max(1)
    if fmt == "e4m3":
        byte = np.frexp(amax)[1] - 1 + 127 - 7
    else:
        mant, ex = np.frexp(amax / 6.0)
        byte = np.where(mant > 0.5, ex, ex - 1) + 127
    byte = np.clip(np.where(amax > 0, byte, 1), 1, 254)
    scaled = (w * np.exp2(127.0 - byte)[:, None, :]).reshape(k, n).astype(np.float32)
    by_word = np.ascontiguousarray(scaled.reshape(k // 512, 128, 4, n).transpose(0, 1, 3, 2))
    if fmt == "e4m3":
        words = by_word.astype(ml_dtypes.float8_e4m3fn).view(np.uint8)
    else:
        c = by_word.astype(ml_dtypes.float4_e2m1fn).view(np.uint8) & 0xF
        words = c[..., 0::2] | (c[..., 1::2] << 4)
    return np.ascontiguousarray(words), np.ascontiguousarray(byte.astype(np.uint8).reshape(k // 512, 16, n))


def unpack_weight(words, scales, fmt):
    g, p, n, _ = words.shape
    if fmt == "e4m3":
        vals = np.ascontiguousarray(words).view(ml_dtypes.float8_e4m3fn).astype(np.float64)
    else:
        nib = np.empty((g, p, n, 4), np.uint8)
        nib[..., 0::2] = words & 0xF
        nib[..., 1::2] = words >> 4
        vals = E2M1[nib]
    vals = vals * np.repeat(np.exp2(scales.astype(np.float64) - 127.0), 8, axis=1)[..., None]
    return vals.transpose(0, 1, 3, 2).reshape(g * 512, n)
def pack4(w):
    words, scales = pack_weight(w, "e2m1")
    return words.reshape(words.shape[0], 128, -1), scales


def unpack4(words, scales):
    return unpack_weight(words.reshape(words.shape[0], 128, -1, 2), scales, "e2m1")


def planes(Y):
    n, m = Y.shape
    b = f64(bf(Y)).reshape(n // 32, 32, m)
    amax = np.abs(b).max(1)
    byte = np.clip(np.where(amax > 0, np.frexp(amax)[1] - 1 + 127 - 7, 1), 1, 254)
    codes = (b * np.exp2(127.0 - byte)[:, None, :]).reshape(n, m).astype(np.float32).astype(ml_dtypes.float8_e4m3fn).view(np.uint8)
    words = codes.reshape(n // 512, 128, 4, m).transpose(0, 1, 3, 2)
    return np.ascontiguousarray(words), np.ascontiguousarray(byte.astype(np.uint8).reshape(n // 512, 16, m))


M, K, N = 1536, 2048, 1024
BASE_SPREAD = 0.4
VAR_FLOOR = 0.1

def randn(*shape):
    return np.random.standard_normal(shape)

def setup_inputs():
    s = mx_kscale(K)
    anomalies = randn(K, M) * s[:, None]
    x_words, x_scales = pack_weight(anomalies, "e4m3")
    var = VAR_FLOOR + np.exp(1.2 * randn(N))
    modes = randn(K, N) * np.sqrt(var / K)[None, :] / s[:, None]
    baseline = BASE_SPREAD * randn(N) * np.sqrt(var)
    month_weight = np.exp(0.3 * randn(M))
    return {"x_words": x_words, "x_scales": x_scales, "modes": bf(modes),
            "mode_var": bf(var), "baseline": bf(baseline),
            "month_weight": bf(month_weight)}

def reference(x_words, x_scales, modes, mode_var, baseline, month_weight):
    A = unpack_weight(x_words, x_scales, "e4m3")
    E = mxq(f64(modes), 0, "e4m3")
    scores = A.T @ E
    departure = scores - f64(baseline)[None, :]
    y = departure / f64(mode_var)[None, :] * f64(month_weight)[:, None]
    Y = y.T
    words, scales = planes(Y)
    return y, words, scales

@@ -1,0 +1,349 @@
+from contextlib import ExitStack
+
+import concourse.mybir as mybir
+from concourse.masks import make_identity
+
+M, K, N = 1536, 2048, 1024
+FLOPS = 2 * M * K * N
+
+F32 = mybir.dt.float32
+BF16 = mybir.dt.bfloat16
+I32 = mybir.dt.int32
+U32 = mybir.dt.uint32
+U8 = mybir.dt.uint8
+FP8X4 = mybir.dt.float8_e4m3fn_x4
+ACT = mybir.ActivationFunctionType
+ALU = mybir.AluOpType
+
+P = 128
+PACK = 4
+GROUP = P * PACK
+PASSES = K // GROUP
+MODE_GROUPS = N // GROUP
+CHUNK = 512
+CHUNKS = M // CHUNK
+M_TILES = M // P
+BANKS = 8
+PAIRS = P // 2
+VECTOR_PAIRS = 40
+UNITS = [(0, 0, 512), (0, 512, 512), (0, 1024, 512), (1, 0, 512), (1, 512, 512),
+         (1, 1024, 256), (1, 1280, 128), (1, 1408, 128)]
+
+
+def tile_variance_divided_mode_scores_g6_kernel(
+    tc, x_words, x_scales, modes, mode_var, baseline, month_weight, out_0, out_1, out_2
+):
+    nc = tc.nc
+    with ExitStack() as ctx:
+        keep = ctx.enter_context(tc.tile_pool(name="keep", bufs=1))
+        work = ctx.enter_context(tc.tile_pool(name="work", bufs=1))
+        psum = ctx.enter_context(tc.psum_pool(name="psum", bufs=1))
+        ctx.enter_context(tc.manual_schedule())
+
+        ring = [0]
+
+        def next_bank(shape, dtype):
+            b = ring[0] % BANKS
+            ring[0] = ring[0] + 1
+            return psum.tile(shape, dtype, tag="bank%d" % b, name="bank%d" % b)
+
+        a_scales = keep.tile([P, M], U8, name="a_scales", align_bytes=256)
+        w_rows = keep.tile([P, P], BF16, name="w_rows", align_bytes=64)
+        ident_f32 = keep.tile([P, P], F32, name="ident_f32", align_bytes=64)
+        ident_bf = keep.tile([P, P], BF16, name="ident_bf", align_bytes=64)
+        var_raw = keep.tile([P, MODE_GROUPS, PACK], BF16, name="var_raw")
+        base_raw = keep.tile([P, MODE_GROUPS, PACK], BF16, name="base_raw")
+        inv_var = keep.tile([P, MODE_GROUPS * PACK], F32, name="inv_var")
+        shift = keep.tile([P, MODE_GROUPS * PACK], F32, name="shift")
+        w_col_bf = keep.tile([P, 16], BF16, name="w_col_bf")
+        w_col = keep.tile([P, 16], F32, name="w_col")
+        w_all = keep.tile([P, M], BF16, name="w_all", align_bytes=64)
+        y_scales = [keep.tile([P, M], U8, name="y_scales%d" % g, align_bytes=256) for g in range(MODE_GROUPS)]
+
+        raw, grouped, e_codes, e_scales, a_codes = {}, {}, {}, {}, {}
+        acc, centred, turned, y_bf, y_rows = {}, {}, {}, {}, {}
+
+        def load_modes(g, kg):
+            raw[g, kg] = keep.tile([P, PACK, GROUP], BF16, name="raw%d%d" % (g, kg), align_bytes=256)
+            rows = modes[kg * GROUP:(kg + 1) * GROUP, g * GROUP:(g + 1) * GROUP]
+            nc.sync.dma_start(out=raw[g, kg][:], in_=rows.rearrange("(p j) n -> p j n", j=PACK))
+
+        def load_a(kg, c):
+            t = keep.tile([P, CHUNK], U32, name="a_front%d%d" % (kg, c), align_bytes=256)
+            src = x_words[kg].rearrange("p n t -> p (n t)")[:, c * CHUNK * PACK:(c + 1) * CHUNK * PACK]
+            nc.sync.dma_start(out=t[:].bitcast(I32), in_=src.bitcast(I32))
+            a_codes[kg, c] = t[:]
+
+        def load_a_back(kg0):
+            t = keep.tile([P, 2, CHUNK], U32, name="a_back%d" % kg0, align_bytes=256)
+            src = x_words[kg0:kg0 + 2].rearrange("g p n t -> p g (n t)")[:, :, 2 * CHUNK * PACK:]
+            nc.sync.dma_start(out=t[:].bitcast(I32), in_=src.bitcast(I32))
+            a_codes[kg0, 2] = t[:, 0, :]
+            a_codes[kg0 + 1, 2] = t[:, 1, :]
+
+        def interleave(g, kg, vector_pairs=PAIRS):
+            grouped[g, kg] = work.tile([P, PACK, P * PACK], BF16, tag="grouped", name="grouped", bufs=3, align_bytes=64)
+            dst = grouped[g, kg][:].rearrange("p t (a i j) -> p a t i j", i=2, j=PACK)
+            src = raw[g, kg][:].rearrange("p j (a i t) -> p a t i j", i=2, t=PACK)
+            nc.vector.tensor_copy(out=dst[:, 0:vector_pairs], in_=src[:, 0:vector_pairs])
+            if vector_pairs < PAIRS:
+                nc.scalar.copy(out=dst[:, vector_pairs:], in_=src[:, vector_pairs:])
+
+        def quantise_modes(g, kg, parts):
+            e_codes[g, kg] = keep.tile([P, GROUP], U32, name="e_codes%d%d" % (g, kg), align_bytes=64)
+            e_scales[g, kg] = keep.tile([P, GROUP], U8, name="e_scales%d%d" % (g, kg), align_bytes=64)
+            flat = grouped[g, kg][:].rearrange("p t c -> p (t c)")
+            w = GROUP // parts
+            for h in range(parts):
+                nc.vector.quantize_mx(
+                    out=e_codes[g, kg][:, h * w:(h + 1) * w].bitcast(FP8X4),
+                    scales=e_scales[g, kg][:, h * w:(h + 1) * w],
+                    in_=flat[:, h * w * PACK:(h + 1) * w * PACK],
+                )
+
+        def mx_pass(u, t, kg):
+            g, m0, width = UNITS[u]
+            c, off = divmod(m0, CHUNK)
+            if kg == 0:
+                acc[u, t] = next_bank([P, width], F32)
+            nc.tensor.matmul_mx(
+                out=acc[u, t][:],
+                lhsT=e_codes[g, kg][:, t * P:(t + 1) * P].bitcast(FP8X4),
+                lhsT_scale=e_scales[g, kg][:, t * P:(t + 1) * P],
+                rhs=a_codes[kg, c][:, off:off + width].bitcast(FP8X4),
+                rhs_scale=a_scales[PACK * kg:, m0:m0 + width],
+                start=(kg == 0),
+                stop=(kg == PASSES - 1),
+            )
+
+        def mx_slot(u, t):
+            for kg in range(PASSES):
+                mx_pass(u, t, kg)
+
+        def centre(u, t, on_vector=False):
+            g, m0, width = UNITS[u]
+            if u not in centred:
+                centred[u] = work.tile([P, PACK, width], F32, tag="centred", name="centred", bufs=5, align_bytes=64)
+            col = slice(g * PACK + t, g * PACK + t + 1)
+            if on_vector:
+                nc.vector.tensor_scalar(out=centred[u][:, t, :], in0=acc[u, t][:], scalar1=inv_var[:, col],
+                                        scalar2=shift[:, col], op0=ALU.mult, op1=ALU.add)
+            else:
+                nc.scalar.activation(out=centred[u][:, t, :], in_=acc[u, t][:], func=ACT.Identity,
+                                     bias=shift[:, col], scale=inv_var[:, col])
+
+        def turn(u, slot_major=False):
+            tiles = UNITS[u][2] // P
+            for i in range(tiles):
+                turned[u, i] = next_bank([P, PACK, P], F32)
+            order = [(i, t) for i in range(tiles) for t in range(PACK)]
+            for i, t in order:
+                nc.tensor.transpose(turned[u, i][:, t, :], centred[u][:, t, i * P:(i + 1) * P], ident_f32[:])
+
+        def weigh_rows(u, i, on_vector=False):
+            g, m0, width = UNITS[u]
+            h, e = divmod(i, 2)
+            if e == 0:
+                y_rows[u, h] = work.tile([P, 2, GROUP], F32, tag="y_rows", name="y_rows", bufs=5, align_bytes=256)
+            dst = y_rows[u, h][:, e, :].rearrange("p (q t) -> p q t", t=PACK)
+            src = turned[u, i][:].rearrange("p t q -> p q t")
+            w = w_col[:, m0 // P + i:m0 // P + i + 1]
+            if on_vector:
+                nc.vector.tensor_scalar(out=dst, in0=src, scalar1=w, scalar2=None, op0=ALU.mult)
+            else:
+                nc.scalar.activation(out=dst, in_=src, func=ACT.Copy, scale=w)
+
+        def store_rows(u, i0, n, queue=nc.sync):
+            g, m0, width = UNITS[u]
+            r0 = m0 + i0 * P
+            dram = out_0[r0:r0 + n * P, g * GROUP:(g + 1) * GROUP].rearrange("(e p) n -> p e n", p=P)
+            queue.dma_start(out=dram, in_=y_rows[u, i0 // 2][:, 0:n, :])
+
+        def weigh_modes(u):
+            g, m0, width = UNITS[u]
+            y_bf[u] = work.tile([P, width * PACK], BF16, tag="y_bf", name="y_bf", bufs=3, align_bytes=64)
+            nc.vector.tensor_tensor(
+                out=y_bf[u][:].rearrange("p (a i t) -> p a t i", i=PACK, t=PACK),
+                in0=centred[u][:].rearrange("p t (a i) -> p a t i", i=PACK),
+                in1=w_all[:, m0:m0 + width].rearrange("p (a i) -> p a i", i=PACK)
+                .unsqueeze(2).to_broadcast([P, width // PACK, PACK, PACK]),
+                op=ALU.mult,
+            )
+
+        def quantise_y(u):
+            g, m0, width = UNITS[u]
+            codes = work.tile([P, width], U32, tag="y_codes", name="y_codes", bufs=3, align_bytes=256)
+            nc.vector.quantize_mx(out=codes[:].bitcast(FP8X4), scales=y_scales[g][:, m0:m0 + width], in_=y_bf[u][:])
+            dram = out_1[g].rearrange("p m t -> p (m t)")[:, m0 * PACK:(m0 + width) * PACK]
+            nc.sync.dma_start(out=dram.bitcast(I32), in_=codes[:].bitcast(I32))
+
+        def store_scales(g):
+            for q in range(4):
+                nc.sync.dma_start(out=out_2[g, 4 * q:4 * q + 4, :].bitcast(I32),
+                                  in_=y_scales[g][32 * q:32 * q + 4, :].bitcast(I32))
+
+        nc.vector.memset(w_rows[:], 0.0)
+        nc.vector.memset(a_scales[:].bitcast(I32), 0)
+        w_view = month_weight.rearrange("(c p) -> c p", p=P)
+        nc.scalar.dma_start(out=w_rows[0:8, :], in_=w_view[0:8, :])
+        nc.scalar.dma_start(out=w_rows[8:12, :], in_=w_view[8:12, :])
+        load_modes(0, 0)
+        for q in range(4):
+            nc.sync.dma_start(out=a_scales[32 * q:32 * q + 16, :].bitcast(I32),
+                              in_=x_scales[:, 4 * q:4 * q + 4, :].bitcast(I32))
+        load_a(0, 0)
+        load_modes(0, 1)
+        load_a(0, 1)
+        load_a(1, 0)
+        load_modes(0, 2)
+        load_a(1, 1)
+        load_a(2, 0)
+        load_modes(0, 3)
+        load_a(2, 1)
+        nc.sync.dma_start(out=var_raw[:], in_=mode_var.rearrange("(g p t) -> p g t", p=P, t=PACK))
+        nc.sync.dma_start(out=base_raw[:], in_=baseline.rearrange("(g p t) -> p g t", p=P, t=PACK))
+        load_a(3, 0)
+        load_a(3, 1)
+        load_modes(1, 0)
+        load_a_back(0)
+        load_a_back(2)
+        for kg in range(1, PASSES):
+            load_modes(1, kg)
+
+        make_identity(nc, ident_f32[:])
+        nc.scalar.activation(out=ident_bf[:], in_=ident_f32[:], func=ACT.Copy)
+
+        ring[0] = 5
+        w_t = next_bank([P, P], BF16)
+        nc.tensor.transpose(w_t[:], w_rows[:], ident_bf[:])
+        nc.scalar.copy(out=w_col_bf[:], in_=w_t[:, 0:16])
+        nc.scalar.copy(out=w_col[:], in_=w_t[:, 0:16])
+        w_spread = [next_bank([P, 8 * P], BF16), next_bank([P, 4 * P], BF16)]
+        for c in range(M_TILES):
+            nc.tensor.transpose(w_spread[c // 8][:, (c % 8) * P:(c % 8 + 1) * P],
+                                w_col_bf[:, c:c + 1].to_broadcast([P, P]), ident_bf[:])
+
+        for kg in range(PASSES):
+            interleave(0, kg, VECTOR_PAIRS)
+            if kg == PASSES - 1:
+                nc.vector.reciprocal(out=inv_var[:], in_=var_raw[:].rearrange("p g t -> p (g t)"))
+            quantise_modes(0, kg, PACK)
+            if kg == 0:
+                nc.scalar.copy(out=w_all[:, 0:8 * P], in_=w_spread[0][:])
+                nc.scalar.copy(out=w_all[:, 8 * P:], in_=w_spread[1][:])
+            if kg == PASSES - 1:
+                nc.vector.scalar_tensor_tensor(out=shift[:], in0=base_raw[:].rearrange("p g t -> p (g t)"),
+                                               scalar=-1.0, in1=inv_var[:], op0=ALU.mult, op1=ALU.mult)
+            for u in (0, 1):
+                for t in range(PACK):
+                    mx_pass(u, t, kg)
+
+        centre(0, 0)
+        centre(0, 1, True)
+        centre(0, 2)
+        centre(0, 3, True)
+        for t in range(PACK):
+            centre(1, t)
+        turn(0)
+        interleave(1, 0)
+        weigh_modes(0)
+        quantise_modes(1, 0, 1)
+        for t in range(PACK):
+            mx_slot(2, t)
+        for i in range(PACK):
+            weigh_rows(0, i)
+        store_rows(0, 0, 2)
+        quantise_y(0)
+        store_rows(0, 2, 2)
+        for t in range(PACK):
+            centre(2, t)
+        turn(1)
+        interleave(1, 1)
+        interleave(1, 2)
+        quantise_modes(1, 1, 1)
+        quantise_modes(1, 2, 1)
+        for kg in (0, 1):
+            for t in range(PACK):
+                mx_pass(3, t, kg)
+        for i in range(PACK):
+            weigh_rows(1, i)
+        store_rows(1, 0, 2)
+        store_rows(1, 2, 2)
+        interleave(1, 3, 40)
+        quantise_modes(1, 3, 1)
+        weigh_modes(1)
+        turn(2)
+        for kg in (2, 3):
+            for t in range(PACK):
+                mx_pass(3, t, kg)
+        for i in range(PACK):
+            weigh_rows(2, i)
+        store_rows(2, 0, 2)
+        store_rows(2, 2, 2)
+        weigh_modes(2)
+        quantise_y(1)
+        for t in range(PACK):
+            centre(3, t)
+        quantise_y(2)
+        store_scales(0)
+        mx_slot(4, 0)
+        mx_slot(4, 1)
+        turn(3)
+        centre(4, 0)
+        centre(4, 1)
+        weigh_modes(3)
+        mx_slot(4, 2)
+        mx_slot(4, 3)
+        weigh_rows(3, 0)
+        weigh_rows(3, 1)
+        store_rows(3, 0, 2)
+        quantise_y(3)
+        centre(4, 2)
+        weigh_rows(3, 2)
+        weigh_rows(3, 3, True)
+        centre(4, 3)
+        store_rows(3, 2, 2)
+        mx_slot(5, 0)
+        mx_slot(5, 1)
+        turn(4)
+        weigh_modes(4)
+        centre(5, 0)
+        centre(5, 1)
+        mx_slot(5, 2)
+        mx_slot(5, 3)
+        weigh_rows(4, 0)
+        weigh_rows(4, 1)
+        store_rows(4, 0, 2)
+        quantise_y(4)
+        centre(5, 2)
+        centre(5, 3)
+        weigh_rows(4, 2)
+        mx_slot(6, 0)
+        mx_slot(6, 1)
+        weigh_rows(4, 3)
+        store_rows(4, 2, 2)
+        mx_slot(6, 2)
+        mx_slot(6, 3)
+        turn(5)
+        weigh_modes(5)
+        for t in range(PACK):
+            centre(6, t)
+        quantise_y(5)
+        weigh_rows(5, 0)
+        for t in range(PACK):
+            mx_slot(7, t)
+        weigh_rows(5, 1, True)
+        store_rows(5, 0, 2)
+        weigh_modes(6)
+        turn(6)
+        for t in range(PACK):
+            centre(7, t)
+        turn(7, True)
+        quantise_y(6)
+        weigh_rows(6, 0)
+        store_rows(6, 0, 1)
+        weigh_modes(7)
+        weigh_rows(7, 0)
+        quantise_y(7)
+        store_rows(7, 0, 1, nc.scalar)
+        store_scales(1)

@@ -47,12 +47,14 @@ def tile_variance_divided_mode_scores_g6_kernel(
             ring[0] = ring[0] + 1
             return psum.tile(shape, dtype, tag="bank%d" % b, name="bank%d" % b)
 
-        a_scales = keep.tile([P, M], U8, name="a_scales", align_bytes=256)
+        a_scales = [keep.tile([P, 2 * CHUNK], U8, name="a_scales_front", align_bytes=256),
+                    keep.tile([P, CHUNK], U8, name="a_scales_back", align_bytes=256)]
         w_rows = keep.tile([P, P], BF16, name="w_rows", align_bytes=64)
         ident_f32 = keep.tile([P, P], F32, name="ident_f32", align_bytes=64)
         ident_bf = keep.tile([P, P], BF16, name="ident_bf", align_bytes=64)
-        var_raw = keep.tile([P, MODE_GROUPS, PACK], BF16, name="var_raw")
-        base_raw = keep.tile([P, MODE_GROUPS, PACK], BF16, name="base_raw")
+        vec_rows = keep.tile([P, MODE_GROUPS * P], BF16, name="vec_rows", align_bytes=64)
+        vec_sorted = keep.tile([P, MODE_GROUPS * P], BF16, name="vec_sorted", align_bytes=64)
+        vec_cols = keep.tile([P, MODE_GROUPS * P], BF16, name="vec_cols", align_bytes=64)
         inv_var = keep.tile([P, MODE_GROUPS * PACK], F32, name="inv_var")
         shift = keep.tile([P, MODE_GROUPS * PACK], F32, name="shift")
         w_col_bf = keep.tile([P, 16], BF16, name="w_col_bf")
@@ -73,6 +75,15 @@ def tile_variance_divided_mode_scores_g6_kernel(
             src = x_words[kg].rearrange("p n t -> p (n t)")[:, c * CHUNK * PACK:(c + 1) * CHUNK * PACK]
             nc.sync.dma_start(out=t[:].bitcast(I32), in_=src.bitcast(I32))
             a_codes[kg, c] = t[:]
+
+        def load_scales(part, m0, width):
+            for q in range(4):
+                nc.sync.dma_start(out=a_scales[part][32 * q:32 * q + 16, :].bitcast(I32),
+                                  in_=x_scales[:, 4 * q:4 * q + 4, m0:m0 + width].bitcast(I32))
+
+        def load_vector(row, vec):
+            nc.sync.dma_start(out=vec_rows[row:P:32, :].rearrange("q (g c) -> q g c", g=MODE_GROUPS),
+                              in_=vec.rearrange("(g q c) -> q g c", g=MODE_GROUPS, q=4))
 
         def load_a_back(kg0):
             t = keep.tile([P, 2, CHUNK], U32, name="a_back%d" % kg0, align_bytes=256)
@@ -111,7 +122,7 @@ def tile_variance_divided_mode_scores_g6_kernel(
                 lhsT=e_codes[g, kg][:, t * P:(t + 1) * P].bitcast(FP8X4),
                 lhsT_scale=e_scales[g, kg][:, t * P:(t + 1) * P],
                 rhs=a_codes[kg, c][:, off:off + width].bitcast(FP8X4),
-                rhs_scale=a_scales[PACK * kg:, m0:m0 + width],
+                rhs_scale=a_scales[c // 2][PACK * kg:, m0 % (2 * CHUNK):m0 % (2 * CHUNK) + width],
                 start=(kg == 0),
                 stop=(kg == PASSES - 1),
             )
@@ -163,10 +174,10 @@ def tile_variance_divided_mode_scores_g6_kernel(
             g, m0, width = UNITS[u]
             y_bf[u] = work.tile([P, width * PACK], BF16, tag="y_bf", name="y_bf", bufs=3, align_bytes=64)
             nc.vector.tensor_tensor(
-                out=y_bf[u][:].rearrange("p (a i t) -> p a t i", i=PACK, t=PACK),
-                in0=centred[u][:].rearrange("p t (a i) -> p a t i", i=PACK),
-                in1=w_all[:, m0:m0 + width].rearrange("p (a i) -> p a i", i=PACK)
-                .unsqueeze(2).to_broadcast([P, width // PACK, PACK, PACK]),
+                out=y_bf[u][:].rearrange("p (a i t) -> p a t i", i=2, t=PACK),
+                in0=centred[u][:].rearrange("p t (a i) -> p a t i", i=2),
+                in1=w_all[:, m0:m0 + width].rearrange("p (a i) -> p a i", i=2)
+                .unsqueeze(2).to_broadcast([P, width // 2, PACK, 2]),
                 op=ALU.mult,
             )
 
@@ -182,42 +193,42 @@ def tile_variance_divided_mode_scores_g6_kernel(
                 nc.sync.dma_start(out=out_2[g, 4 * q:4 * q + 4, :].bitcast(I32),
                                   in_=y_scales[g][32 * q:32 * q + 4, :].bitcast(I32))
 
-        nc.vector.memset(w_rows[:], 0.0)
-        nc.vector.memset(a_scales[:].bitcast(I32), 0)
+        nc.gpsimd.memset(w_rows[:], 0.0)
+        nc.vector.memset(a_scales[0][:].bitcast(I32), 0)
+        nc.vector.memset(a_scales[1][:].bitcast(I32), 0)
+        nc.vector.memset(vec_rows[:], 0.0)
         w_view = month_weight.rearrange("(c p) -> c p", p=P)
         nc.scalar.dma_start(out=w_rows[0:8, :], in_=w_view[0:8, :])
         nc.scalar.dma_start(out=w_rows[8:12, :], in_=w_view[8:12, :])
         load_modes(0, 0)
-        for q in range(4):
-            nc.sync.dma_start(out=a_scales[32 * q:32 * q + 16, :].bitcast(I32),
-                              in_=x_scales[:, 4 * q:4 * q + 4, :].bitcast(I32))
+        load_scales(0, 0, 2 * CHUNK)
         load_a(0, 0)
         load_modes(0, 1)
         load_a(0, 1)
         load_a(1, 0)
+        load_vector(0, mode_var)
+        load_vector(1, baseline)
         load_modes(0, 2)
         load_a(1, 1)
         load_a(2, 0)
         load_modes(0, 3)
         load_a(2, 1)
-        nc.sync.dma_start(out=var_raw[:], in_=mode_var.rearrange("(g p t) -> p g t", p=P, t=PACK))
-        nc.sync.dma_start(out=base_raw[:], in_=baseline.rearrange("(g p t) -> p g t", p=P, t=PACK))
         load_a(3, 0)
         load_a(3, 1)
-        load_modes(1, 0)
+        load_scales(1, 2 * CHUNK, CHUNK)
         load_a_back(0)
         load_a_back(2)
-        for kg in range(1, PASSES):
+        for kg in range(PASSES):
             load_modes(1, kg)
 
+        make_identity(nc, ident_bf[:])
         make_identity(nc, ident_f32[:])
-        nc.scalar.activation(out=ident_bf[:], in_=ident_f32[:], func=ACT.Copy)
 
         ring[0] = 5
         w_t = next_bank([P, P], BF16)
         nc.tensor.transpose(w_t[:], w_rows[:], ident_bf[:])
-        nc.scalar.copy(out=w_col_bf[:], in_=w_t[:, 0:16])
-        nc.scalar.copy(out=w_col[:], in_=w_t[:, 0:16])
+        nc.vector.tensor_copy(out=w_col_bf[:], in_=w_t[:, 0:16])
+        nc.scalar.activation(out=w_col[:], in_=w_t[:, 0:16], func=ACT.Copy)
         w_spread = [next_bank([P, 8 * P], BF16), next_bank([P, 4 * P], BF16)]
         for c in range(M_TILES):
             nc.tensor.transpose(w_spread[c // 8][:, (c % 8) * P:(c % 8 + 1) * P],
@@ -225,14 +236,19 @@ def tile_variance_divided_mode_scores_g6_kernel(
 
         for kg in range(PASSES):
             interleave(0, kg, VECTOR_PAIRS)
-            if kg == PASSES - 1:
-                nc.vector.reciprocal(out=inv_var[:], in_=var_raw[:].rearrange("p g t -> p (g t)"))
+            if kg == 2:
+                nc.vector.tensor_copy(out=vec_sorted[:].rearrange("p (g t i) -> p g t i", t=PACK, i=32),
+                                      in_=vec_rows[:].rearrange("p (g i t) -> p g t i", t=PACK, i=32))
+            if kg == 3:
+                nc.vector.reciprocal(out=inv_var[:], in_=vec_cols[:, 0:MODE_GROUPS * P:32])
             quantise_modes(0, kg, PACK)
             if kg == 0:
                 nc.scalar.copy(out=w_all[:, 0:8 * P], in_=w_spread[0][:])
                 nc.scalar.copy(out=w_all[:, 8 * P:], in_=w_spread[1][:])
-            if kg == PASSES - 1:
-                nc.vector.scalar_tensor_tensor(out=shift[:], in0=base_raw[:].rearrange("p g t -> p (g t)"),
+            if kg == 2:
+                nc.vector.transpose(out=vec_cols[:], in_=vec_sorted[:])
+            if kg == 3:
+                nc.vector.scalar_tensor_tensor(out=shift[:], in0=vec_cols[:, 1:MODE_GROUPS * P:32],
                                                scalar=-1.0, in1=inv_var[:], op0=ALU.mult, op1=ALU.mult)
             for u in (0, 1):
                 for t in range(PACK):
@@ -245,15 +261,15 @@ def tile_variance_divided_mode_scores_g6_kernel(
         for t in range(PACK):
             centre(1, t)
         turn(0)
-        interleave(1, 0)
         weigh_modes(0)
-        quantise_modes(1, 0, 1)
+        interleave(1, 0)
         for t in range(PACK):
             mx_slot(2, t)
         for i in range(PACK):
             weigh_rows(0, i)
         store_rows(0, 0, 2)
         quantise_y(0)
+        quantise_modes(1, 0, 1)
         store_rows(0, 2, 2)
         for t in range(PACK):
             centre(2, t)

from contextlib import ExitStack

import concourse.mybir as mybir
from concourse.masks import make_identity

M, K, N = 1536, 2048, 1024
FLOPS = 2 * M * K * N

F32 = mybir.dt.float32
BF16 = mybir.dt.bfloat16
I32 = mybir.dt.int32
U32 = mybir.dt.uint32
U8 = mybir.dt.uint8
FP8X4 = mybir.dt.float8_e4m3fn_x4
ACT = mybir.ActivationFunctionType
ALU = mybir.AluOpType

P = 128
PACK = 4
GROUP = P * PACK
PASSES = K // GROUP
MODE_GROUPS = N // GROUP
CHUNK = 512
CHUNKS = M // CHUNK
M_TILES = M // P
BANKS = 8
PAIRS = P // 2
VECTOR_PAIRS = 40
UNITS = [(0, 0, 512), (0, 512, 512), (0, 1024, 512), (1, 0, 512), (1, 512, 512),
         (1, 1024, 256), (1, 1280, 128), (1, 1408, 128)]


def tile_variance_divided_mode_scores_g6_kernel(
    tc, x_words, x_scales, modes, mode_var, baseline, month_weight, out_0, out_1, out_2
):
    nc = tc.nc
    with ExitStack() as ctx:
        keep = ctx.enter_context(tc.tile_pool(name="keep", bufs=1))
        work = ctx.enter_context(tc.tile_pool(name="work", bufs=1))
        psum = ctx.enter_context(tc.psum_pool(name="psum", bufs=1))
        ctx.enter_context(tc.manual_schedule())

        ring = [0]

        def next_bank(shape, dtype):
            b = ring[0] % BANKS
            ring[0] = ring[0] + 1
            return psum.tile(shape, dtype, tag="bank%d" % b, name="bank%d" % b)

        a_scales = [keep.tile([P, 2 * CHUNK], U8, name="a_scales_front", align_bytes=256),
                    keep.tile([P, CHUNK], U8, name="a_scales_back", align_bytes=256)]
        w_rows = keep.tile([P, P], BF16, name="w_rows", align_bytes=64)
        ident_f32 = keep.tile([P, P], F32, name="ident_f32", align_bytes=64)
        ident_bf = keep.tile([P, P], BF16, name="ident_bf", align_bytes=64)
        vec_rows = keep.tile([P, MODE_GROUPS * P], BF16, name="vec_rows", align_bytes=64)
        vec_sorted = keep.tile([P, MODE_GROUPS * P], BF16, name="vec_sorted", align_bytes=64)
        vec_cols = keep.tile([P, MODE_GROUPS * P], BF16, name="vec_cols", align_bytes=64)
        inv_var = keep.tile([P, MODE_GROUPS * PACK], F32, name="inv_var")
        shift = keep.tile([P, MODE_GROUPS * PACK], F32, name="shift")
        w_col_bf = keep.tile([P, 16], BF16, name="w_col_bf")
        w_col = keep.tile([P, 16], F32, name="w_col")
        w_all = keep.tile([P, M], BF16, name="w_all", align_bytes=64)
        y_scales = [keep.tile([P, M], U8, name="y_scales%d" % g, align_bytes=256) for g in range(MODE_GROUPS)]

        raw, grouped, e_codes, e_scales, a_codes = {}, {}, {}, {}, {}
        acc, centred, turned, y_bf, y_rows = {}, {}, {}, {}, {}

        def load_modes(g, kg):
            raw[g, kg] = keep.tile([P, PACK, GROUP], BF16, name="raw%d%d" % (g, kg), align_bytes=256)
            rows = modes[kg * GROUP:(kg + 1) * GROUP, g * GROUP:(g + 1) * GROUP]
            nc.sync.dma_start(out=raw[g, kg][:], in_=rows.rearrange("(p j) n -> p j n", j=PACK))

        def load_a(kg, c):
            t = keep.tile([P, CHUNK], U32, name="a_front%d%d" % (kg, c), align_bytes=256)
            src = x_words[kg].rearrange("p n t -> p (n t)")[:, c * CHUNK * PACK:(c + 1) * CHUNK * PACK]
            nc.sync.dma_start(out=t[:].bitcast(I32), in_=src.bitcast(I32))
            a_codes[kg, c] = t[:]

        def load_scales(part, m0, width):
            for q in range(4):
                nc.sync.dma_start(out=a_scales[part][32 * q:32 * q + 16, :].bitcast(I32),
                                  in_=x_scales[:, 4 * q:4 * q + 4, m0:m0 + width].bitcast(I32))

        def load_vector(row, vec):
            nc.sync.dma_start(out=vec_rows[row:P:32, :].rearrange("q (g c) -> q g c", g=MODE_GROUPS),
                              in_=vec.rearrange("(g q c) -> q g c", g=MODE_GROUPS, q=4))

        def load_a_back(kg0):
            t = keep.tile([P, 2, CHUNK], U32, name="a_back%d" % kg0, align_bytes=256)
            src = x_words[kg0:kg0 + 2].rearrange("g p n t -> p g (n t)")[:, :, 2 * CHUNK * PACK:]
            nc.sync.dma_start(out=t[:].bitcast(I32), in_=src.bitcast(I32))
            a_codes[kg0, 2] = t[:, 0, :]
            a_codes[kg0 + 1, 2] = t[:, 1, :]

        def interleave(g, kg, vector_pairs=PAIRS):
            grouped[g, kg] = work.tile([P, PACK, P * PACK], BF16, tag="grouped", name="grouped", bufs=3, align_bytes=64)
            dst = grouped[g, kg][:].rearrange("p t (a i j) -> p a t i j", i=2, j=PACK)
            src = raw[g, kg][:].rearrange("p j (a i t) -> p a t i j", i=2, t=PACK)
            nc.vector.tensor_copy(out=dst[:, 0:vector_pairs], in_=src[:, 0:vector_pairs])
            if vector_pairs < PAIRS:
                nc.scalar.copy(out=dst[:, vector_pairs:], in_=src[:, vector_pairs:])

        def quantise_modes(g, kg, parts):
            e_codes[g, kg] = keep.tile([P, GROUP], U32, name="e_codes%d%d" % (g, kg), align_bytes=64)
            e_scales[g, kg] = keep.tile([P, GROUP], U8, name="e_scales%d%d" % (g, kg), align_bytes=64)
            flat = grouped[g, kg][:].rearrange("p t c -> p (t c)")
            w = GROUP // parts
            for h in range(parts):
                nc.vector.quantize_mx(
                    out=e_codes[g, kg][:, h * w:(h + 1) * w].bitcast(FP8X4),
                    scales=e_scales[g, kg][:, h * w:(h + 1) * w],
                    in_=flat[:, h * w * PACK:(h + 1) * w * PACK],
                )

        def mx_pass(u, t, kg):
            g, m0, width = UNITS[u]
            c, off = divmod(m0, CHUNK)
            if kg == 0:
                acc[u, t] = next_bank([P, width], F32)
            nc.tensor.matmul_mx(
                out=acc[u, t][:],
                lhsT=e_codes[g, kg][:, t * P:(t + 1) * P].bitcast(FP8X4),
                lhsT_scale=e_scales[g, kg][:, t * P:(t + 1) * P],
                rhs=a_codes[kg, c][:, off:off + width].bitcast(FP8X4),
                rhs_scale=a_scales[c // 2][PACK * kg:, m0 % (2 * CHUNK):m0 % (2 * CHUNK) + width],
                start=(kg == 0),
                stop=(kg == PASSES - 1),
            )

        def mx_slot(u, t):
            for kg in range(PASSES):
                mx_pass(u, t, kg)

        def centre(u, t, on_vector=False):
            g, m0, width = UNITS[u]
            if u not in centred:
                centred[u] = work.tile([P, PACK, width], F32, tag="centred", name="centred", bufs=5, align_bytes=64)
            col = slice(g * PACK + t, g * PACK + t + 1)
            if on_vector:
                nc.vector.tensor_scalar(out=centred[u][:, t, :], in0=acc[u, t][:], scalar1=inv_var[:, col],
                                        scalar2=shift[:, col], op0=ALU.mult, op1=ALU.add)
            else:
                nc.scalar.activation(out=centred[u][:, t, :], in_=acc[u, t][:], func=ACT.Identity,
                                     bias=shift[:, col], scale=inv_var[:, col])

        def turn(u, slot_major=False):
            tiles = UNITS[u][2] // P
            for i in range(tiles):
                turned[u, i] = next_bank([P, PACK, P], F32)
            order = [(i, t) for i in range(tiles) for t in range(PACK)]
            for i, t in order:
                nc.tensor.transpose(turned[u, i][:, t, :], centred[u][:, t, i * P:(i + 1) * P], ident_f32[:])

        def weigh_rows(u, i, on_vector=False):
            g, m0, width = UNITS[u]
            h, e = divmod(i, 2)
            if e == 0:
                y_rows[u, h] = work.tile([P, 2, GROUP], F32, tag="y_rows", name="y_rows", bufs=5, align_bytes=256)
            dst = y_rows[u, h][:, e, :].rearrange("p (q t) -> p q t", t=PACK)
            src = turned[u, i][:].rearrange("p t q -> p q t")
            w = w_col[:, m0 // P + i:m0 // P + i + 1]
            if on_vector:
                nc.vector.tensor_scalar(out=dst, in0=src, scalar1=w, scalar2=None, op0=ALU.mult)
            else:
                nc.scalar.activation(out=dst, in_=src, func=ACT.Copy, scale=w)

        def store_rows(u, i0, n, queue=nc.sync):
            g, m0, width = UNITS[u]
            r0 = m0 + i0 * P
            dram = out_0[r0:r0 + n * P, g * GROUP:(g + 1) * GROUP].rearrange("(e p) n -> p e n", p=P)
            queue.dma_start(out=dram, in_=y_rows[u, i0 // 2][:, 0:n, :])

        def weigh_modes(u):
            g, m0, width = UNITS[u]
            y_bf[u] = work.tile([P, width * PACK], BF16, tag="y_bf", name="y_bf", bufs=3, align_bytes=64)
            nc.vector.tensor_tensor(
                out=y_bf[u][:].rearrange("p (a i t) -> p a t i", i=2, t=PACK),
                in0=centred[u][:].rearrange("p t (a i) -> p a t i", i=2),
                in1=w_all[:, m0:m0 + width].rearrange("p (a i) -> p a i", i=2)
                .unsqueeze(2).to_broadcast([P, width // 2, PACK, 2]),
                op=ALU.mult,
            )

        def quantise_y(u):
            g, m0, width = UNITS[u]
            codes = work.tile([P, width], U32, tag="y_codes", name="y_codes", bufs=3, align_bytes=256)
            nc.vector.quantize_mx(out=codes[:].bitcast(FP8X4), scales=y_scales[g][:, m0:m0 + width], in_=y_bf[u][:])
            dram = out_1[g].rearrange("p m t -> p (m t)")[:, m0 * PACK:(m0 + width) * PACK]
            nc.sync.dma_start(out=dram.bitcast(I32), in_=codes[:].bitcast(I32))

        def store_scales(g):
            for q in range(4):
                nc.sync.dma_start(out=out_2[g, 4 * q:4 * q + 4, :].bitcast(I32),
                                  in_=y_scales[g][32 * q:32 * q + 4, :].bitcast(I32))

        nc.gpsimd.memset(w_rows[:], 0.0)
        nc.vector.memset(a_scales[0][:].bitcast(I32), 0)
        nc.vector.memset(a_scales[1][:].bitcast(I32), 0)
        nc.vector.memset(vec_rows[:], 0.0)
        w_view = month_weight.rearrange("(c p) -> c p", p=P)
        nc.scalar.dma_start(out=w_rows[0:8, :], in_=w_view[0:8, :])
        nc.scalar.dma_start(out=w_rows[8:12, :], in_=w_view[8:12, :])
        load_modes(0, 0)
        load_scales(0, 0, 2 * CHUNK)
        load_a(0, 0)
        load_modes(0, 1)
        load_a(0, 1)
        load_a(1, 0)
        load_vector(0, mode_var)
        load_vector(1, baseline)
        load_modes(0, 2)
        load_a(1, 1)
        load_a(2, 0)
        load_modes(0, 3)
        load_a(2, 1)
        load_a(3, 0)
        load_a(3, 1)
        load_scales(1, 2 * CHUNK, CHUNK)
        load_a_back(0)
        load_a_back(2)
        for kg in range(PASSES):
            load_modes(1, kg)

        make_identity(nc, ident_bf[:])
        make_identity(nc, ident_f32[:])

        ring[0] = 5
        w_t = next_bank([P, P], BF16)
        nc.tensor.transpose(w_t[:], w_rows[:], ident_bf[:])
        nc.vector.tensor_copy(out=w_col_bf[:], in_=w_t[:, 0:16])
        nc.scalar.activation(out=w_col[:], in_=w_t[:, 0:16], func=ACT.Copy)
        w_spread = [next_bank([P, 8 * P], BF16), next_bank([P, 4 * P], BF16)]
        for c in range(M_TILES):
            nc.tensor.transpose(w_spread[c // 8][:, (c % 8) * P:(c % 8 + 1) * P],
                                w_col_bf[:, c:c + 1].to_broadcast([P, P]), ident_bf[:])

        for kg in range(PASSES):
            interleave(0, kg, VECTOR_PAIRS)
            if kg == 2:
                nc.vector.tensor_copy(out=vec_sorted[:].rearrange("p (g t i) -> p g t i", t=PACK, i=32),
                                      in_=vec_rows[:].rearrange("p (g i t) -> p g t i", t=PACK, i=32))
            if kg == 3:
                nc.vector.reciprocal(out=inv_var[:], in_=vec_cols[:, 0:MODE_GROUPS * P:32])
            quantise_modes(0, kg, PACK)
            if kg == 0:
                nc.scalar.copy(out=w_all[:, 0:8 * P], in_=w_spread[0][:])
                nc.scalar.copy(out=w_all[:, 8 * P:], in_=w_spread[1][:])
            if kg == 2:
                nc.vector.transpose(out=vec_cols[:], in_=vec_sorted[:])
            if kg == 3:
                nc.vector.scalar_tensor_tensor(out=shift[:], in0=vec_cols[:, 1:MODE_GROUPS * P:32],
                                               scalar=-1.0, in1=inv_var[:], op0=ALU.mult, op1=ALU.mult)
            for u in (0, 1):
                for t in range(PACK):
                    mx_pass(u, t, kg)

        centre(0, 0)
        centre(0, 1, True)
        centre(0, 2)
        centre(0, 3, True)
        for t in range(PACK):
            centre(1, t)
        turn(0)
        weigh_modes(0)
        interleave(1, 0)
        for t in range(PACK):
            mx_slot(2, t)
        for i in range(PACK):
            weigh_rows(0, i)
        store_rows(0, 0, 2)
        quantise_y(0)
        quantise_modes(1, 0, 1)
        store_rows(0, 2, 2)
        for t in range(PACK):
            centre(2, t)
        turn(1)
        interleave(1, 1)
        interleave(1, 2)
        quantise_modes(1, 1, 1)
        quantise_modes(1, 2, 1)
        for kg in (0, 1):
            for t in range(PACK):
                mx_pass(3, t, kg)
        for i in range(PACK):
            weigh_rows(1, i)
        store_rows(1, 0, 2)
        store_rows(1, 2, 2)
        interleave(1, 3, 40)
        quantise_modes(1, 3, 1)
        weigh_modes(1)
        turn(2)
        for kg in (2, 3):
            for t in range(PACK):
                mx_pass(3, t, kg)
        for i in range(PACK):
            weigh_rows(2, i)
        store_rows(2, 0, 2)
        store_rows(2, 2, 2)
        weigh_modes(2)
        quantise_y(1)
        for t in range(PACK):
            centre(3, t)
        quantise_y(2)
        store_scales(0)
        mx_slot(4, 0)
        mx_slot(4, 1)
        turn(3)
        centre(4, 0)
        centre(4, 1)
        weigh_modes(3)
        mx_slot(4, 2)
        mx_slot(4, 3)
        weigh_rows(3, 0)
        weigh_rows(3, 1)
        store_rows(3, 0, 2)
        quantise_y(3)
        centre(4, 2)
        weigh_rows(3, 2)
        weigh_rows(3, 3, True)
        centre(4, 3)
        store_rows(3, 2, 2)
        mx_slot(5, 0)
        mx_slot(5, 1)
        turn(4)
        weigh_modes(4)
        centre(5, 0)
        centre(5, 1)
        mx_slot(5, 2)
        mx_slot(5, 3)
        weigh_rows(4, 0)
        weigh_rows(4, 1)
        store_rows(4, 0, 2)
        quantise_y(4)
        centre(5, 2)
        centre(5, 3)
        weigh_rows(4, 2)
        mx_slot(6, 0)
        mx_slot(6, 1)
        weigh_rows(4, 3)
        store_rows(4, 2, 2)
        mx_slot(6, 2)
        mx_slot(6, 3)
        turn(5)
        weigh_modes(5)
        for t in range(PACK):
            centre(6, t)
        quantise_y(5)
        weigh_rows(5, 0)
        for t in range(PACK):
            mx_slot(7, t)
        weigh_rows(5, 1, True)
        store_rows(5, 0, 2)
        weigh_modes(6)
        turn(6)
        for t in range(PACK):
            centre(7, t)
        turn(7, True)
        quantise_y(6)
        weigh_rows(6, 0)
        store_rows(6, 0, 1)
        weigh_modes(7)
        weigh_rows(7, 0)
        quantise_y(7)
        store_rows(7, 0, 1, nc.scalar)
        store_scales(1)
